import numpy as np
import ml_dtypes


def mxq(x, axis, fmt="e4m3"):
    dtype, down = {"e4m3": (ml_dtypes.float8_e4m3fn, 7), "e5m2": (ml_dtypes.float8_e5m2, 14)}[fmt]
    v = np.moveaxis(np.asarray(x, np.float32).astype(ml_dtypes.bfloat16).astype(np.float64), axis, -1)
    blocks = v.reshape(v.shape[:-1] + (-1, 32))
    amax = np.abs(blocks).max(-1, keepdims=True)
    byte = np.maximum(np.where(amax > 0, np.frexp(amax)[1] - 1 + 127, 0) - down, 1)
    scale = np.exp2(byte - 127.0)
    codes = (blocks / scale).astype(np.float32).astype(dtype).astype(np.float64)
    return np.moveaxis((codes * scale).reshape(v.shape), -1, axis)


WIDE = False


def mx_kscale(k):
    if not WIDE:
        return np.ones(k)
    levels = np.array([10, -10, 5, -5, 0])
    if k % 512:
        return np.exp2(np.random.permutation(np.resize(levels, k // 32))).repeat(32)
    a = np.empty((k // 512, 16))
    for p in range(k // 512):
        a[p, :8] = np.random.permutation(np.resize(levels, 8))
        for g in range(8):
            far = levels[np.abs(levels - a[p, g]) >= 10]
            a[p, g + 8] = far[np.random.randint(len(far))]
    return np.exp2(a.ravel()).repeat(32)


def f64(x):
    return np.asarray(x).astype(np.float64)


def striped(idx):
    return np.tile(idx.reshape(-1, 16).T, (8, 1)).astype(np.uint16)


def unstriped(offs):
    return offs[:16].T.reshape(-1).astype(np.int64)


def striped8(idx):
    return np.concatenate([x.reshape(-1, 16).T for x in idx]).astype(np.uint16)


def runs(offs, k):
    lists = np.stack([offs[16 * r : 16 * r + 16].T.reshape(-1) for r in range(8)]).astype(np.int64)
    return lists[np.arange(k) % 512 // 64]


def pack_weight(w):
    k, n = w.shape
    w = f64(np.asarray(w, np.float32).astype(ml_dtypes.bfloat16)).reshape(k // 32, 32, n)
    amax = np.abs(w).max(1)
    byte = np.clip(np.where(amax > 0, np.frexp(amax)[1] - 1 + 127 - 7, 1), 1, 254)
    scaled = (w * np.exp2(127.0 - byte)[:, None, :]).reshape(k, n).astype(np.float32)
    words = np.ascontiguousarray(scaled.reshape(k // 512, 128, 4, n).transpose(0, 1, 3, 2)).astype(ml_dtypes.float8_e4m3fn).view(np.uint8)
    return words, np.ascontiguousarray(byte.astype(np.uint8).reshape(k // 512, 16, n))


def unpack_weight(words, scales):
    g, p, n, _ = words.shape
    vals = np.ascontiguousarray(words).view(ml_dtypes.float8_e4m3fn).astype(np.float64) * np.repeat(np.exp2(scales.astype(np.float64) - 127.0), 8, axis=1)[..., None]
    return vals.transpose(0, 1, 3, 2).reshape(g * 512, n)

def planes(y):
    n, m = y.shape
    v = y.astype(np.float32).astype(ml_dtypes.bfloat16).astype(np.float64).reshape(n // 32, 32, m)
    top = np.abs(v).max(1)
    byte = np.clip(np.where(top > 0, np.frexp(top)[1] - 1 + 127 - 7, 1), 1, 254)
    codes = (v * np.exp2(127.0 - byte)[:, None, :]).reshape(n, m).astype(np.float32).astype(ml_dtypes.float8_e4m3fn).view(np.uint8)
    words = codes.reshape(n // 512, 128, 4, m).transpose(0, 1, 3, 2)
    return np.ascontiguousarray(words), np.ascontiguousarray(byte.astype(np.uint8).reshape(n // 512, 16, m))


K, T, S, G, H, W = 512, 1024, 512, 2048, 512, 256


def setup_inputs():
    n = np.random.standard_normal
    s = mx_kscale(K)[:, None]
    packed_xT = pack_weight(n((K, T)) * s)
    packed_dT = pack_weight(n((K, G)) / s)
    perm = np.stack([np.random.permutation(S) for _ in range(8)])
    return {
        "x_words": packed_xT[0],
        "x_scales": packed_xT[1],
        "d_words": packed_dT[0],
        "d_scales": packed_dT[1],
        "gs": (np.random.uniform(0.5, 1.5, (K, 1)) * s).astype(np.float32),
        "offs": striped(np.random.permutation(T)[:S]),
        "k1": striped8(np.random.randint(0, G, (8, H))),
        "n1": striped8(np.stack([np.random.permutation(S) for _ in range(8)])),
        "n2": striped8(np.stack([np.random.permutation(S) for _ in range(8)])),
        "k2": striped8(np.random.randint(0, G, (8, H))),
        "n3": striped8(perm[:, :W]),
        "n4": striped8(perm[:, W:]),
    }


def reference(x_words, x_scales, d_words, d_scales, gs, offs, k1, n1, n2, k2, n3, n4):
    d_k2 = unpack_weight(d_words, d_scales)[np.arange(K)[:, None], runs(k2, K)]
    d_k1 = unpack_weight(d_words, d_scales)[np.arange(K)[:, None], runs(k1, K)]
    xq = unpack_weight(x_words, x_scales)[:, unstriped(offs)]
    h = 0.0625 * (d_k1.T @ xq)
    z = f64(gs) * (h * (h[np.arange(H)[:, None], runs(n1, H)] - (h[np.arange(H)[:, None], runs(n2, H)])))
    h2 = 0.0625 * ((d_k2.T @ mxq(z, 0, "e4m3")))
    pa = h2[np.arange(H)[:, None], runs(n3, H)]
    pb = h2[np.arange(H)[:, None], runs(n4, H)]
    rb = np.minimum(pa, pb)
    ra = np.maximum(pa, pb)
    ds = np.zeros((H, S))
    ds[np.arange(H)[:, None], runs(n3, H)] = ra
    out = ds.copy()
    out[np.arange(H)[:, None], runs(n4, H)] = rb
    return (out,) + planes(out)

@@ -1,0 +1,221 @@
+from contextlib import ExitStack
+
+import concourse.mybir as mybir
+
+F32 = mybir.dt.float32
+BF16 = mybir.dt.bfloat16
+I32 = mybir.dt.int32
+U32 = mybir.dt.uint32
+U16 = mybir.dt.uint16
+U8 = mybir.dt.uint8
+FP8X4 = mybir.dt.float8_e4m3fn_x4
+ALU = mybir.AluOpType
+ACT = mybir.ActivationFunctionType
+
+P = 128
+PACK = 4
+T, G, S, H, W = 1024, 2048, 512, 512, 256
+HALF = S // 2
+FLOPS = 2 * 2 * 512 * H * S
+
+
+def tile_picked_codewindorder_none_po_kernel(
+    tc, x_words, x_scales, d_words, d_scales, gs, offs, k1, n1, n2, k2, n3, n4, out_0, out_1, out_2
+):
+    nc = tc.nc
+    with ExitStack() as ctx:
+        lists = ctx.enter_context(tc.tile_pool(name="lists", bufs=1))
+        keep = ctx.enter_context(tc.tile_pool(name="keep", bufs=1))
+        psum = ctx.enter_context(tc.psum_pool(name="psum", bufs=1))
+
+        def sb(name, shape, dtype):
+            return keep.tile(shape, dtype, name=name, align_bytes=64)
+
+        def load_list(name, src):
+            tile = lists.tile(list(src.shape), U16, name=name)
+            nc.sync.dma_start(tile[:], src)
+            return tile
+
+        d_sc = sb("d_sc", [P, G], U8)
+        x_sc = sb("x_sc", [P, T], U8)
+        nc.vector.memset(d_sc[:].bitcast(I32), 0)
+        nc.vector.memset(x_sc[:].bitcast(I32), 0)
+        placed1 = sb("placed1", [P, H + S], U8)
+        placed2 = sb("placed2", [P, H], U8)
+        nc.gpsimd.memset(placed1[:].bitcast(I32), 0)
+        nc.gpsimd.memset(placed2[:].bitcast(I32), 0)
+
+        k1_t = load_list("k1_t", k1)
+        nc.scalar.dma_start(d_sc[0:P:8, :].bitcast(I32), d_scales[0].bitcast(I32))
+        offs_t = load_list("offs_t", offs)
+        nc.scalar.dma_start(x_sc[0:P:8, :].bitcast(I32), x_scales[0].bitcast(I32))
+        x_w = sb("x_w", [P, T], U32)
+        d_w = sb("d_w", [P, G], U32)
+        nc.sync.dma_start(x_w[:].bitcast(I32), x_words[0].rearrange("p c r -> p (c r)").bitcast(I32))
+        nc.sync.dma_start(d_w[:].bitcast(I32), d_words[0].rearrange("p c r -> p (c r)").bitcast(I32))
+        k2_t = load_list("k2_t", k2)
+        gs_t = sb("gs_t", [P, PACK], F32)
+        nc.sync.dma_start(gs_t[:], gs.rearrange("(p t) o -> p (t o)", t=PACK))
+        n1_t = load_list("n1_t", n1)
+        n2_t = load_list("n2_t", n2)
+        n3_t = load_list("n3_t", n3)
+        n4_t = load_list("n4_t", n4)
+
+        gain = sb("gain", [P, PACK], F32)
+        nc.scalar.activation(gain[:], gs_t[:], ACT.Copy, scale=-0.0625 * 0.0625)
+
+        def place_rows(placed, picked, queues):
+            for j in range(PACK):
+                queues[j % len(queues)].dma_start(placed[j:P:32, :].bitcast(I32), picked[8 * j : P : 32, :].bitcast(I32))
+
+        def deal(name, src, dtype):
+            dealt = sb(name, [P, H], dtype)
+            nc.vector.tensor_copy(dealt[:].rearrange("p (t m) -> p t m", t=PACK), src.rearrange("p (m t) -> p t m", t=PACK))
+            return dealt
+
+        picked1 = sb("picked1", [P, H + S], U8)
+        nc.vector.tensor_copy(picked1[:, 0:H], d_sc[:].indirect(k1_t[:]))
+        nc.vector.tensor_copy(picked1[:, H : H + S], x_sc[:].indirect(offs_t[:]))
+        place_rows(placed1, picked1, [nc.sync, nc.scalar])
+        xq_w = sb("xq_w", [P, S], U32)
+        nc.vector.tensor_copy(xq_w[:], x_w[:].indirect(offs_t[:]))
+        w1_picked = sb("w1_picked", [P, H], U32)
+        nc.vector.tensor_copy(w1_picked[:], d_w[:].indirect(k1_t[:]))
+        w1_sc = deal("w1_sc", placed1[:, 0:H], U8)
+        w1_w = deal("w1_w", w1_picked[:], U32)
+
+        h_win = [sb(f"h_win{t}", [P, S], F32) for t in range(PACK)]
+        h_raw = sb("h_raw", [P, PACK, S], F32)
+        acc1 = [psum.tile([P, S], F32, name=f"acc1_{t}", tag=f"bank{t}") for t in range(PACK)]
+        for t in range(PACK):
+            cols = slice(t * P, (t + 1) * P)
+            nc.tensor.matmul_mx(
+                acc1[t][:], lhsT=w1_w[:, cols].bitcast(FP8X4), lhsT_scale=w1_sc[:, cols],
+                rhs=xq_w[:].bitcast(FP8X4), rhs_scale=placed1[:, H : H + S], start=True, stop=True,
+            )
+            nc.scalar.activation(h_win[t][:], acc1[t][:], ACT.Copy, scale=gain[:, t : t + 1])
+        for t in range(PACK):
+            nc.scalar.copy(h_raw[:, t, :], acc1[t][:])
+
+        picked2 = sb("picked2", [P, H], U8)
+        nc.vector.tensor_copy(picked2[:], d_sc[:].indirect(k2_t[:]))
+        place_rows(placed2, picked2, [nc.sync])
+        w2_picked = sb("w2_picked", [P, H], U32)
+        nc.vector.tensor_copy(w2_picked[:], d_w[:].indirect(k2_t[:]))
+        w2_w = deal("w2_w", w2_picked[:], U32)
+
+        h2_win = [sb(f"h2_win{t}", [P, S], F32) for t in range(PACK)]
+        first = [sb(f"first{c}", [P, PACK, HALF], F32) for c in range(2)]
+        diff = [sb(f"diff{c}", [P, PACK, HALF], F32) for c in range(2)]
+        z_bf = [sb(f"z_bf{c}", [P, HALF, PACK], BF16) for c in range(2)]
+        z_w = [sb(f"z_w{c}", [P, HALF], U32) for c in range(2)]
+        z_sc = [sb(f"z_sc{c}", [P, HALF], U8) for c in range(2)]
+        per = HALF // 16
+
+        def fetch_first(c, t):
+            nc.vector.tensor_copy(first[c][:, t, :], h_win[t][:].indirect(n1_t[:, c * per : (c + 1) * per]))
+
+        def fetch_diff(c, t):
+            nc.vector.tensor_tensor(
+                diff[c][:, t, :], h_win[t][:].indirect(n2_t[:, c * per : (c + 1) * per]), first[c][:, t, :], ALU.subtract
+            )
+
+        def make_z(c):
+            nc.vector.tensor_tensor(
+                z_bf[c][:].rearrange("p (a i) t -> p a t i", i=2),
+                diff[c][:].rearrange("p t (a i) -> p a t i", i=2),
+                h_raw[:, :, c * HALF : (c + 1) * HALF].rearrange("p t (a i) -> p a t i", i=2),
+                ALU.mult,
+            )
+
+        def quantize_z(c):
+            nc.vector.quantize_mx(z_w[c][:].bitcast(FP8X4), z_sc[c][:], z_bf[c][:].rearrange("p c t -> p (c t)"))
+
+        def second_product(c):
+            for t in range(PACK):
+                cols = slice(t * P, (t + 1) * P)
+                acc2 = psum.tile([P, HALF], F32, name=f"acc2_{c}_{t}", tag=f"bank{(1 - c) * PACK + t}")
+                nc.tensor.matmul_mx(
+                    acc2[:], lhsT=w2_w[:, cols].bitcast(FP8X4), lhsT_scale=w2_sc[:, cols],
+                    rhs=z_w[c][:].bitcast(FP8X4), rhs_scale=z_sc[c][:], start=True, stop=True,
+                )
+                nc.scalar.activation(h2_win[t][:, c * HALF : (c + 1) * HALF], acc2[:], ACT.Copy, scale=0.0625)
+
+        fetch_first(0, 0)
+        for t in range(1, PACK):
+            fetch_first(0, t)
+            fetch_diff(0, t - 1)
+        fetch_first(1, 0)
+        fetch_diff(0, PACK - 1)
+        fetch_first(1, 1)
+        make_z(0)
+        fetch_diff(1, 0)
+        quantize_z(0)
+        w2_sc = deal("w2_sc", placed2[:], U8)
+        second_product(0)
+        for t in range(2, PACK):
+            fetch_first(1, t)
+            fetch_diff(1, t - 1)
+        fetch_diff(1, PACK - 1)
+        make_z(1)
+        quantize_z(1)
+        second_product(1)
+
+        pa = [sb(f"pa{t}", [P, W], F32) for t in range(PACK)]
+        gap = [sb(f"gap{t}", [P, W], F32) for t in range(PACK)]
+        up = [sb(f"up{t}", [P, W], F32) for t in range(PACK)]
+        neg = [sb(f"neg{t}", [P, W], F32) for t in range(PACK)]
+        down = [sb(f"down{t}", [P, W], F32) for t in range(PACK)]
+        y = [sb(f"y{t}", [P, S], F32) for t in range(PACK)]
+        y_bf = sb("y_bf", [P, S, PACK], BF16)
+        y_w = sb("y_w", [P, S], U32)
+        y_sc = sb("y_sc", [P, S], U8)
+        out_rows = out_0.rearrange("(p t) c -> p t c", t=PACK)
+
+        def fetch_pa(t):
+            nc.vector.tensor_copy(pa[t][:], h2_win[t][:].indirect(n3_t[:]))
+
+        def fetch_gap(t):
+            nc.vector.tensor_tensor(gap[t][:], h2_win[t][:].indirect(n4_t[:]), pa[t][:], ALU.subtract)
+            nc.scalar.activation(up[t][:], gap[t][:], ACT.Relu)
+            nc.scalar.activation(neg[t][:], gap[t][:], ACT.Relu, scale=-1.0)
+            nc.scalar.activation(down[t][:], neg[t][:], ACT.Copy, scale=-1.0)
+
+        def put_larger(t):
+            nc.vector.tensor_tensor(y[t][:].indirect(n3_t[:]), pa[t][:], up[t][:], ALU.add)
+
+        def put_smaller(t):
+            nc.vector.tensor_tensor(y[t][:].indirect(n4_t[:]), pa[t][:], down[t][:], ALU.add)
+            nc.sync.dma_start(out_rows[:, t, :], y[t][:])
+
+        fetch_pa(0)
+        fetch_pa(1)
+        fetch_gap(0)
+        fetch_gap(1)
+        fetch_pa(2)
+        fetch_pa(3)
+        put_larger(0)
+        put_larger(1)
+        put_smaller(0)
+        nc.scalar.copy(y_bf[:, :, 0], y[0][:])
+        fetch_gap(2)
+        fetch_gap(3)
+        put_smaller(1)
+        nc.scalar.copy(y_bf[:, :, 1], y[1][:])
+        put_larger(2)
+        put_larger(3)
+        put_smaller(2)
+        nc.scalar.copy(y_bf[:, :, 2:4], y[2][:].unsqueeze(2).to_broadcast([P, S, 2]))
+        put_smaller(3)
+        words_out = out_1[0].rearrange("p c r -> p (c r)").bitcast(I32)
+        for c in range(2):
+            cols = slice(c * HALF, (c + 1) * HALF)
+            nc.vector.tensor_copy(y_bf[:, cols, 3], y[3][:, cols])
+        for c in range(2):
+            cols = slice(c * HALF, (c + 1) * HALF)
+            nc.vector.quantize_mx(y_w[:, cols].bitcast(FP8X4), y_sc[:, cols], y_bf[:, cols, :].rearrange("p c t -> p (c t)"))
+            nc.sync.dma_start(words_out[:, cols], y_w[:, cols].bitcast(I32))
+        scales_out = out_2[0].bitcast(I32)
+        for q in range(4):
+            queue = nc.scalar if q % 2 == 0 else nc.sync
+            queue.dma_start(scales_out[4 * q : 4 * q + 4, :], y_sc[32 * q : 32 * q + 4, :].bitcast(I32))

@@ -28,8 +28,8 @@ def tile_picked_codewindorder_none_po_kernel(
         keep = ctx.enter_context(tc.tile_pool(name="keep", bufs=1))
         psum = ctx.enter_context(tc.psum_pool(name="psum", bufs=1))
 
-        def sb(name, shape, dtype):
-            return keep.tile(shape, dtype, name=name, align_bytes=64)
+        def sb(name, shape, dtype, tag=None):
+            return keep.tile(shape, dtype, name=name, tag=tag or name, align_bytes=64)
 
         def load_list(name, src):
             tile = lists.tile(list(src.shape), U16, name=name)
@@ -38,25 +38,23 @@ def tile_picked_codewindorder_none_po_kernel(
 
         d_sc = sb("d_sc", [P, G], U8)
         x_sc = sb("x_sc", [P, T], U8)
-        nc.vector.memset(d_sc[:].bitcast(I32), 0)
-        nc.vector.memset(x_sc[:].bitcast(I32), 0)
         placed1 = sb("placed1", [P, H + S], U8)
         placed2 = sb("placed2", [P, H], U8)
         nc.gpsimd.memset(placed1[:].bitcast(I32), 0)
         nc.gpsimd.memset(placed2[:].bitcast(I32), 0)
 
-        k1_t = load_list("k1_t", k1)
-        nc.scalar.dma_start(d_sc[0:P:8, :].bitcast(I32), d_scales[0].bitcast(I32))
         offs_t = load_list("offs_t", offs)
-        nc.scalar.dma_start(x_sc[0:P:8, :].bitcast(I32), x_scales[0].bitcast(I32))
+        nc.scalar.dma_start(x_sc[:].bitcast(I32), x_scales[0].bitcast(I32).unsqueeze(1).to_broadcast([16, 8, T // 4]))
+        k1_t = load_list("k1_t", k1)
+        nc.sync.dma_start(d_sc[:].bitcast(I32), d_scales[0].bitcast(I32).unsqueeze(1).to_broadcast([16, 8, G // 4]))
         x_w = sb("x_w", [P, T], U32)
         d_w = sb("d_w", [P, G], U32)
         nc.sync.dma_start(x_w[:].bitcast(I32), x_words[0].rearrange("p c r -> p (c r)").bitcast(I32))
-        nc.sync.dma_start(d_w[:].bitcast(I32), d_words[0].rearrange("p c r -> p (c r)").bitcast(I32))
         k2_t = load_list("k2_t", k2)
+        n1_t = load_list("n1_t", n1)
         gs_t = sb("gs_t", [P, PACK], F32)
         nc.sync.dma_start(gs_t[:], gs.rearrange("(p t) o -> p (t o)", t=PACK))
-        n1_t = load_list("n1_t", n1)
+        nc.sync.dma_start(d_w[:].bitcast(I32), d_words[0].rearrange("p c r -> p (c r)").bitcast(I32))
         n2_t = load_list("n2_t", n2)
         n3_t = load_list("n3_t", n3)
         n4_t = load_list("n4_t", n4)
@@ -73,9 +71,9 @@ def tile_picked_codewindorder_none_po_kernel(
             nc.vector.tensor_copy(dealt[:].rearrange("p (t m) -> p t m", t=PACK), src.rearrange("p (m t) -> p t m", t=PACK))
             return dealt
 
-        picked1 = sb("picked1", [P, H + S], U8)
-        nc.vector.tensor_copy(picked1[:, 0:H], d_sc[:].indirect(k1_t[:]))
+        picked1 = sb("picked1", [P, H + S], U8, tag="picked")
         nc.vector.tensor_copy(picked1[:, H : H + S], x_sc[:].indirect(offs_t[:]))
+        nc.vector.tensor_copy(picked1[:, 0:H], d_sc[:].indirect(k1_t[:]))
         place_rows(placed1, picked1, [nc.sync, nc.scalar])
         xq_w = sb("xq_w", [P, S], U32)
         nc.vector.tensor_copy(xq_w[:], x_w[:].indirect(offs_t[:]))
@@ -100,46 +98,51 @@ def tile_picked_codewindorder_none_po_kernel(
         picked2 = sb("picked2", [P, H], U8)
         nc.vector.tensor_copy(picked2[:], d_sc[:].indirect(k2_t[:]))
         place_rows(placed2, picked2, [nc.sync])
-        w2_picked = sb("w2_picked", [P, H], U32)
+        w2_picked = sb("w2_picked", [P, H], U32, tag="picked")
         nc.vector.tensor_copy(w2_picked[:], d_w[:].indirect(k2_t[:]))
         w2_w = deal("w2_w", w2_picked[:], U32)
 
         h2_win = [sb(f"h2_win{t}", [P, S], F32) for t in range(PACK)]
         first = [sb(f"first{c}", [P, PACK, HALF], F32) for c in range(2)]
-        diff = [sb(f"diff{c}", [P, PACK, HALF], F32) for c in range(2)]
-        z_bf = [sb(f"z_bf{c}", [P, HALF, PACK], BF16) for c in range(2)]
-        z_w = [sb(f"z_w{c}", [P, HALF], U32) for c in range(2)]
-        z_sc = [sb(f"z_sc{c}", [P, HALF], U8) for c in range(2)]
+        diff = {}
+        pieces = [(0, HALF), (HALF, HALF // 2), (HALF + HALF // 2, HALF // 2)]
+        z_bf = [sb(f"z_bf{n}", [P, width, PACK], BF16) for n, (at, width) in enumerate(pieces)]
+        z_w = [sb(f"z_w{n}", [P, width], U32) for n, (at, width) in enumerate(pieces)]
+        z_sc = [sb(f"z_sc{n}", [P, width], U8) for n, (at, width) in enumerate(pieces)]
         per = HALF // 16
 
         def fetch_first(c, t):
             nc.vector.tensor_copy(first[c][:, t, :], h_win[t][:].indirect(n1_t[:, c * per : (c + 1) * per]))
 
         def fetch_diff(c, t):
+            if c not in diff:
+                diff.setdefault(c, sb(f"diff{c}", [P, PACK, HALF], F32, tag="diff"))
             nc.vector.tensor_tensor(
                 diff[c][:, t, :], h_win[t][:].indirect(n2_t[:, c * per : (c + 1) * per]), first[c][:, t, :], ALU.subtract
             )
 
-        def make_z(c):
+        def make_z(n):
+            at, width = pieces[n]
             nc.vector.tensor_tensor(
-                z_bf[c][:].rearrange("p (a i) t -> p a t i", i=2),
-                diff[c][:].rearrange("p t (a i) -> p a t i", i=2),
-                h_raw[:, :, c * HALF : (c + 1) * HALF].rearrange("p t (a i) -> p a t i", i=2),
+                z_bf[n][:].rearrange("p (a i) t -> p a t i", i=2),
+                diff[at // HALF][:, :, at % HALF : at % HALF + width].rearrange("p t (a i) -> p a t i", i=2),
+                h_raw[:, :, at : at + width].rearrange("p t (a i) -> p a t i", i=2),
                 ALU.mult,
             )
 
-        def quantize_z(c):
-            nc.vector.quantize_mx(z_w[c][:].bitcast(FP8X4), z_sc[c][:], z_bf[c][:].rearrange("p c t -> p (c t)"))
+        def quantize_z(n):
+            nc.vector.quantize_mx(z_w[n][:].bitcast(FP8X4), z_sc[n][:], z_bf[n][:].rearrange("p c t -> p (c t)"))
 
-        def second_product(c):
+        def second_product(n):
+            at, width = pieces[n]
             for t in range(PACK):
                 cols = slice(t * P, (t + 1) * P)
-                acc2 = psum.tile([P, HALF], F32, name=f"acc2_{c}_{t}", tag=f"bank{(1 - c) * PACK + t}")
+                acc2 = psum.tile([P, width], F32, name=f"acc2_{n}_{t}", tag=f"bank{(n + 1) % 2 * PACK + t}")
                 nc.tensor.matmul_mx(
                     acc2[:], lhsT=w2_w[:, cols].bitcast(FP8X4), lhsT_scale=w2_sc[:, cols],
-                    rhs=z_w[c][:].bitcast(FP8X4), rhs_scale=z_sc[c][:], start=True, stop=True,
+                    rhs=z_w[n][:].bitcast(FP8X4), rhs_scale=z_sc[n][:], start=True, stop=True,
                 )
-                nc.scalar.activation(h2_win[t][:, c * HALF : (c + 1) * HALF], acc2[:], ACT.Copy, scale=0.0625)
+                nc.scalar.activation(h2_win[t][:, at : at + width], acc2[:], ACT.Copy, scale=0.0625)
 
         fetch_first(0, 0)
         for t in range(1, PACK):
@@ -147,19 +150,21 @@ def tile_picked_codewindorder_none_po_kernel(
             fetch_diff(0, t - 1)
         fetch_first(1, 0)
         fetch_diff(0, PACK - 1)
-        fetch_first(1, 1)
+        for t in range(1, PACK):
+            fetch_first(1, t)
         make_z(0)
         fetch_diff(1, 0)
         quantize_z(0)
         w2_sc = deal("w2_sc", placed2[:], U8)
         second_product(0)
-        for t in range(2, PACK):
-            fetch_first(1, t)
-            fetch_diff(1, t - 1)
-        fetch_diff(1, PACK - 1)
+        for t in range(1, PACK):
+            fetch_diff(1, t)
         make_z(1)
+        make_z(2)
         quantize_z(1)
         second_product(1)
+        quantize_z(2)
+        second_product(2)
 
         pa = [sb(f"pa{t}", [P, W], F32) for t in range(PACK)]
         gap = [sb(f"gap{t}", [P, W], F32) for t in range(PACK)]

@@ -1,6 +1,7 @@
 from contextlib import ExitStack
 
 import concourse.mybir as mybir
+from concourse.masks import make_identity
 
 F32 = mybir.dt.float32
 BF16 = mybir.dt.bfloat16
@@ -43,6 +44,9 @@ def tile_picked_codewindorder_none_po_kernel(
         nc.gpsimd.memset(placed1[:].bitcast(I32), 0)
         nc.gpsimd.memset(placed2[:].bitcast(I32), 0)
 
+        ident = sb("ident", [P, P], F32)
+        make_identity(nc, ident[:])
+
         offs_t = load_list("offs_t", offs)
         nc.scalar.dma_start(x_sc[:].bitcast(I32), x_scales[0].bitcast(I32).unsqueeze(1).to_broadcast([16, 8, T // 4]))
         k1_t = load_list("k1_t", k1)
@@ -66,10 +70,13 @@ def tile_picked_codewindorder_none_po_kernel(
             for j in range(PACK):
                 queues[j % len(queues)].dma_start(placed[j:P:32, :].bitcast(I32), picked[8 * j : P : 32, :].bitcast(I32))
 
-        def deal(name, src, dtype):
-            dealt = sb(name, [P, H], dtype)
-            nc.vector.tensor_copy(dealt[:].rearrange("p (t m) -> p t m", t=PACK), src.rearrange("p (m t) -> p t m", t=PACK))
-            return dealt
+        def deal(name, src, dtype, t0, t1, tag=None):
+            dealt = sb(name, [P, (t1 - t0) * P], dtype, tag=tag)
+            nc.vector.tensor_copy(
+                dealt[:].rearrange("p (t a i) -> p a t i", t=t1 - t0, i=4),
+                src.rearrange("p (a i t) -> p a t i", t=PACK, i=4)[:, :, t0:t1, :],
+            )
+            return [dealt[:, t * P : (t + 1) * P] for t in range(t1 - t0)]
 
         picked1 = sb("picked1", [P, H + S], U8, tag="picked")
         nc.vector.tensor_copy(picked1[:, H : H + S], x_sc[:].indirect(offs_t[:]))
@@ -79,92 +86,94 @@ def tile_picked_codewindorder_none_po_kernel(
         nc.vector.tensor_copy(xq_w[:], x_w[:].indirect(offs_t[:]))
         w1_picked = sb("w1_picked", [P, H], U32)
         nc.vector.tensor_copy(w1_picked[:], d_w[:].indirect(k1_t[:]))
-        w1_sc = deal("w1_sc", placed1[:, 0:H], U8)
-        w1_w = deal("w1_w", w1_picked[:], U32)
+        w1_sc = deal("w1_sc_0", placed1[:, 0:H], U8, 0, 1)
+        w1_w = deal("w1_w_0", w1_picked[:], U32, 0, 1)
+        w1_sc = w1_sc + deal("w1_sc_rest", placed1[:, 0:H], U8, 1, PACK)
+        w1_w = w1_w + deal("w1_w_rest", w1_picked[:], U32, 1, PACK)
 
         h_win = [sb(f"h_win{t}", [P, S], F32) for t in range(PACK)]
-        h_raw = sb("h_raw", [P, PACK, S], F32)
+        plus_a = [sb(f"plus_a{t}", [P, HALF], F32) for t in range(PACK)]
+        minus_a = sb("minus_a", [P, PACK, HALF], F32)
+        plus_b = sb("plus_b", [P, PACK, HALF], F32)
         acc1 = [psum.tile([P, S], F32, name=f"acc1_{t}", tag=f"bank{t}") for t in range(PACK)]
         for t in range(PACK):
-            cols = slice(t * P, (t + 1) * P)
             nc.tensor.matmul_mx(
-                acc1[t][:], lhsT=w1_w[:, cols].bitcast(FP8X4), lhsT_scale=w1_sc[:, cols],
+                acc1[t][:], lhsT=w1_w[t].bitcast(FP8X4), lhsT_scale=w1_sc[t],
                 rhs=xq_w[:].bitcast(FP8X4), rhs_scale=placed1[:, H : H + S], start=True, stop=True,
             )
             nc.scalar.activation(h_win[t][:], acc1[t][:], ACT.Copy, scale=gain[:, t : t + 1])
+            nc.scalar.copy(plus_a[t][:], acc1[t][:, 0:HALF])
+            nc.scalar.activation(minus_a[:, t, :], acc1[t][:, 0:HALF], ACT.Copy, scale=-1.0)
         for t in range(PACK):
-            nc.scalar.copy(h_raw[:, t, :], acc1[t][:])
+            nc.scalar.copy(plus_b[:, t, :], acc1[t][:, HALF:S])
 
         picked2 = sb("picked2", [P, H], U8)
         nc.vector.tensor_copy(picked2[:], d_sc[:].indirect(k2_t[:]))
         place_rows(placed2, picked2, [nc.sync])
         w2_picked = sb("w2_picked", [P, H], U32, tag="picked")
         nc.vector.tensor_copy(w2_picked[:], d_w[:].indirect(k2_t[:]))
-        w2_w = deal("w2_w", w2_picked[:], U32)
+        w2_w = deal("w2_w_0", w2_picked[:], U32, 0, 1)
+        w2_sc = deal("w2_sc_0", placed2[:], U8, 0, 1)
 
         h2_win = [sb(f"h2_win{t}", [P, S], F32) for t in range(PACK)]
-        first = [sb(f"first{c}", [P, PACK, HALF], F32) for c in range(2)]
-        diff = {}
-        pieces = [(0, HALF), (HALF, HALF // 2), (HALF + HALF // 2, HALF // 2)]
-        z_bf = [sb(f"z_bf{n}", [P, width, PACK], BF16) for n, (at, width) in enumerate(pieces)]
-        z_w = [sb(f"z_w{n}", [P, width], U32) for n, (at, width) in enumerate(pieces)]
-        z_sc = [sb(f"z_sc{n}", [P, width], U8) for n, (at, width) in enumerate(pieces)]
+        z_bf = [sb(f"z_bf{n}", [P, P, PACK], BF16) for n in range(4)]
+        z_w = sb("z_w", [P, S], U32)
+        z_sc = sb("z_sc", [P, S], U8)
         per = HALF // 16
 
-        def fetch_first(c, t):
-            nc.vector.tensor_copy(first[c][:, t, :], h_win[t][:].indirect(n1_t[:, c * per : (c + 1) * per]))
+        def quantize_z(n):
+            cols = slice(n * P, (n + 1) * P)
+            nc.vector.quantize_mx(z_w[:, cols].bitcast(FP8X4), z_sc[:, cols], z_bf[n][:].rearrange("p c t -> p (c t)"))
 
-        def fetch_diff(c, t):
-            if c not in diff:
-                diff.setdefault(c, sb(f"diff{c}", [P, PACK, HALF], F32, tag="diff"))
-            nc.vector.tensor_tensor(
-                diff[c][:, t, :], h_win[t][:].indirect(n2_t[:, c * per : (c + 1) * per]), first[c][:, t, :], ALU.subtract
+        def second_product(t, at, width, bank):
+            acc2 = psum.tile([P, width], F32, name=f"acc2_{t}_{at}", tag=f"bank{bank}")
+            nc.tensor.matmul_mx(
+                acc2[:], lhsT=w2_w[t].bitcast(FP8X4), lhsT_scale=w2_sc[t],
+                rhs=z_w[:, at : at + width].bitcast(FP8X4), rhs_scale=z_sc[:, at : at + width], start=True, stop=True,
             )
+            nc.scalar.activation(h2_win[t][:, at : at + width], acc2[:], ACT.Copy, scale=0.0625)
 
-        def make_z(n):
-            at, width = pieces[n]
+        first = sb("first", [P, PACK, HALF], F32)
+        turned = [psum.tile([P, PACK, P], F32, name=f"turned{b}", tag=f"bank{PACK + b}") for b in range(2)]
+        for t in range(PACK):
+            nc.vector.tensor_copy(first[:, t, :], h_win[t][:].indirect(n1_t[:, per : 2 * per]))
+            at_n2 = sb(f"at_n2_{t}", [P, HALF], F32)
+            at_n1 = sb(f"at_n1_{t}", [P, HALF], F32)
+            nc.vector.tensor_tensor(at_n2[:], h_win[t][:].indirect(n2_t[:, 0:per]), plus_a[t][:], ALU.mult)
+            nc.vector.tensor_tensor(at_n1[:], h_win[t][:].indirect(n1_t[:, 0:per]), minus_a[:, t, :], ALU.mult)
+            for b in range(2):
+                cols = slice(b * P, (b + 1) * P)
+                nc.tensor.matmul(turned[b][:, t, :], at_n2[:, cols], ident[:], start=True, stop=False, is_transpose=True)
+                nc.tensor.matmul(turned[b][:, t, :], at_n1[:, cols], ident[:], start=False, stop=True, is_transpose=True)
+        for b in range(2):
+            pairs = sb(f"pairs{b}", [P, 2, P, 2], BF16)
+            nc.scalar.copy(pairs[:], turned[b][:].rearrange("j (u e) p -> j u p e", e=2))
+            words = pairs[:].rearrange("j u p e -> j (u p e)").bitcast(F32)
+            back = psum.tile([P, 2, P], F32, name=f"back{b}", tag=f"bank{6 + b}")
+            for u in range(2):
+                nc.tensor.transpose(back[:, u, :], words[:, u * P : (u + 1) * P], ident[:])
+            nc.scalar.copy(
+                z_bf[b][:].rearrange("p c t -> p (c t)").bitcast(F32).rearrange("p (j u) -> p j u", u=2),
+                back[:].rearrange("p u j -> p j u"),
+            )
+        diff = sb("diff", [P, PACK, HALF], F32, tag="minus_a")
+        for t in range(PACK):
+            nc.vector.tensor_tensor(diff[:, t, :], h_win[t][:].indirect(n2_t[:, per : 2 * per]), first[:, t, :], ALU.subtract)
+        for b in range(2):
+            cols = slice(b * P, (b + 1) * P)
             nc.vector.tensor_tensor(
-                z_bf[n][:].rearrange("p (a i) t -> p a t i", i=2),
-                diff[at // HALF][:, :, at % HALF : at % HALF + width].rearrange("p t (a i) -> p a t i", i=2),
-                h_raw[:, :, at : at + width].rearrange("p t (a i) -> p a t i", i=2),
+                z_bf[2 + b][:].rearrange("p (a i) t -> p a t i", i=2),
+                diff[:, :, cols].rearrange("p t (a i) -> p a t i", i=2),
+                plus_b[:, :, cols].rearrange("p t (a i) -> p a t i", i=2),
                 ALU.mult,
             )
-
-        def quantize_z(n):
-            nc.vector.quantize_mx(z_w[n][:].bitcast(FP8X4), z_sc[n][:], z_bf[n][:].rearrange("p c t -> p (c t)"))
-
-        def second_product(n):
-            at, width = pieces[n]
-            for t in range(PACK):
-                cols = slice(t * P, (t + 1) * P)
-                acc2 = psum.tile([P, width], F32, name=f"acc2_{n}_{t}", tag=f"bank{(n + 1) % 2 * PACK + t}")
-                nc.tensor.matmul_mx(
-                    acc2[:], lhsT=w2_w[:, cols].bitcast(FP8X4), lhsT_scale=w2_sc[:, cols],
-                    rhs=z_w[n][:].bitcast(FP8X4), rhs_scale=z_sc[n][:], start=True, stop=True,
-                )
-                nc.scalar.activation(h2_win[t][:, at : at + width], acc2[:], ACT.Copy, scale=0.0625)
-
-        fetch_first(0, 0)
-        for t in range(1, PACK):
-            fetch_first(0, t)
-            fetch_diff(0, t - 1)
-        fetch_first(1, 0)
-        fetch_diff(0, PACK - 1)
-        for t in range(1, PACK):
-            fetch_first(1, t)
-        make_z(0)
-        fetch_diff(1, 0)
-        quantize_z(0)
-        w2_sc = deal("w2_sc", placed2[:], U8)
-        second_product(0)
-        for t in range(1, PACK):
-            fetch_diff(1, t)
-        make_z(1)
-        make_z(2)
-        quantize_z(1)
-        second_product(1)
-        quantize_z(2)
-        second_product(2)
+        for n, bank in ((2, 0), (3, 1), (0, 4), (1, 5)):
+            quantize_z(n)
+            second_product(0, n * P, P, bank)
+        w2_w = w2_w + deal("w2_w_rest", w2_picked[:], U32, 1, PACK, tag="z_bf1")
+        w2_sc = w2_sc + deal("w2_sc_rest", placed2[:], U8, 1, PACK, tag="z_bf0")
+        for t, bank in ((1, 2), (2, 3), (3, 6)):
+            second_product(t, 0, S, bank)
 
         pa = [sb(f"pa{t}", [P, W], F32) for t in range(PACK)]
         gap = [sb(f"gap{t}", [P, W], F32) for t in range(PACK)]
@@ -177,12 +186,17 @@ def tile_picked_codewindorder_none_po_kernel(
         y_sc = sb("y_sc", [P, S], U8)
         out_rows = out_0.rearrange("(p t) c -> p t c", t=PACK)
 
-        def fetch_pa(t):
-            nc.vector.tensor_copy(pa[t][:], h2_win[t][:].indirect(n3_t[:]))
+        def fetch_pair(t):
+            halves = [(slice(c * P, (c + 1) * P), slice(c * P // 16, (c + 1) * P // 16)) for c in range(2)]
+            for cols, entries in halves:
+                nc.vector.tensor_copy(pa[t][:, cols], h2_win[t][:].indirect(n3_t[:, entries]))
+            for cols, entries in halves:
+                nc.vector.tensor_tensor(gap[t][:, cols], h2_win[t][:].indirect(n4_t[:, entries]), pa[t][:, cols], ALU.subtract)
 
-        def fetch_gap(t):
-            nc.vector.tensor_tensor(gap[t][:], h2_win[t][:].indirect(n4_t[:]), pa[t][:], ALU.subtract)
+        def rise(t):
             nc.scalar.activation(up[t][:], gap[t][:], ACT.Relu)
+
+        def fall(t):
             nc.scalar.activation(neg[t][:], gap[t][:], ACT.Relu, scale=-1.0)
             nc.scalar.activation(down[t][:], neg[t][:], ACT.Copy, scale=-1.0)
 
@@ -193,29 +207,32 @@ def tile_picked_codewindorder_none_po_kernel(
             nc.vector.tensor_tensor(y[t][:].indirect(n4_t[:]), pa[t][:], down[t][:], ALU.add)
             nc.sync.dma_start(out_rows[:, t, :], y[t][:])
 
-        fetch_pa(0)
-        fetch_pa(1)
-        fetch_gap(0)
-        fetch_gap(1)
-        fetch_pa(2)
-        fetch_pa(3)
+        for t in range(PACK):
+            fetch_pair(t)
+        rise(0)
+        for t in range(1, PACK):
+            rise(t)
+            fall(t - 1)
+        fall(PACK - 1)
         put_larger(0)
         put_larger(1)
         put_smaller(0)
         nc.scalar.copy(y_bf[:, :, 0], y[0][:])
-        fetch_gap(2)
-        fetch_gap(3)
+        put_larger(2)
         put_smaller(1)
         nc.scalar.copy(y_bf[:, :, 1], y[1][:])
-        put_larger(2)
         put_larger(3)
         put_smaller(2)
-        nc.scalar.copy(y_bf[:, :, 2:4], y[2][:].unsqueeze(2).to_broadcast([P, S, 2]))
+        split = S - P
+        for cols in (slice(0, HALF), slice(HALF, split)):
+            width = cols.stop - cols.start
+            nc.scalar.copy(y_bf[:, cols, 2:4], y[2][:, cols].unsqueeze(2).to_broadcast([P, width, 2]))
+        nc.scalar.copy(y_bf[:, split:S, 2], y[2][:, split:S])
         put_smaller(3)
         words_out = out_1[0].rearrange("p c r -> p (c r)").bitcast(I32)
-        for c in range(2):
-            cols = slice(c * HALF, (c + 1) * HALF)
+        for cols in (slice(0, HALF), slice(HALF, split)):
             nc.vector.tensor_copy(y_bf[:, cols, 3], y[3][:, cols])
+        nc.scalar.copy(y_bf[:, split:S, 3], y[3][:, split:S])
         for c in range(2):
             cols = slice(c * HALF, (c + 1) * HALF)
             nc.vector.quantize_mx(y_w[:, cols].bitcast(FP8X4), y_sc[:, cols], y_bf[:, cols, :].rearrange("p c t -> p (c t)"))

from contextlib import ExitStack

import concourse.mybir as mybir
from concourse.masks import make_identity

F32 = mybir.dt.float32
BF16 = mybir.dt.bfloat16
I32 = mybir.dt.int32
U32 = mybir.dt.uint32
U16 = mybir.dt.uint16
U8 = mybir.dt.uint8
FP8X4 = mybir.dt.float8_e4m3fn_x4
ALU = mybir.AluOpType
ACT = mybir.ActivationFunctionType

P = 128
PACK = 4
T, G, S, H, W = 1024, 2048, 512, 512, 256
HALF = S // 2
FLOPS = 2 * 2 * 512 * H * S


def tile_picked_codewindorder_none_po_kernel(
    tc, x_words, x_scales, d_words, d_scales, gs, offs, k1, n1, n2, k2, n3, n4, out_0, out_1, out_2
):
    nc = tc.nc
    with ExitStack() as ctx:
        lists = ctx.enter_context(tc.tile_pool(name="lists", bufs=1))
        keep = ctx.enter_context(tc.tile_pool(name="keep", bufs=1))
        psum = ctx.enter_context(tc.psum_pool(name="psum", bufs=1))

        def sb(name, shape, dtype, tag=None):
            return keep.tile(shape, dtype, name=name, tag=tag or name, align_bytes=64)

        def load_list(name, src):
            tile = lists.tile(list(src.shape), U16, name=name)
            nc.sync.dma_start(tile[:], src)
            return tile

        d_sc = sb("d_sc", [P, G], U8)
        x_sc = sb("x_sc", [P, T], U8)
        placed1 = sb("placed1", [P, H + S], U8)
        placed2 = sb("placed2", [P, H], U8)
        nc.gpsimd.memset(placed1[:].bitcast(I32), 0)
        nc.gpsimd.memset(placed2[:].bitcast(I32), 0)

        ident = sb("ident", [P, P], F32)
        make_identity(nc, ident[:])

        offs_t = load_list("offs_t", offs)
        nc.scalar.dma_start(x_sc[:].bitcast(I32), x_scales[0].bitcast(I32).unsqueeze(1).to_broadcast([16, 8, T // 4]))
        k1_t = load_list("k1_t", k1)
        nc.sync.dma_start(d_sc[:].bitcast(I32), d_scales[0].bitcast(I32).unsqueeze(1).to_broadcast([16, 8, G // 4]))
        x_w = sb("x_w", [P, T], U32)
        d_w = sb("d_w", [P, G], U32)
        nc.sync.dma_start(x_w[:].bitcast(I32), x_words[0].rearrange("p c r -> p (c r)").bitcast(I32))
        k2_t = load_list("k2_t", k2)
        n1_t = load_list("n1_t", n1)
        gs_t = sb("gs_t", [P, PACK], F32)
        nc.sync.dma_start(gs_t[:], gs.rearrange("(p t) o -> p (t o)", t=PACK))
        nc.sync.dma_start(d_w[:].bitcast(I32), d_words[0].rearrange("p c r -> p (c r)").bitcast(I32))
        n2_t = load_list("n2_t", n2)
        n3_t = load_list("n3_t", n3)
        n4_t = load_list("n4_t", n4)

        gain = sb("gain", [P, PACK], F32)
        nc.scalar.activation(gain[:], gs_t[:], ACT.Copy, scale=-0.0625 * 0.0625)

        def place_rows(placed, picked, queues):
            for j in range(PACK):
                queues[j % len(queues)].dma_start(placed[j:P:32, :].bitcast(I32), picked[8 * j : P : 32, :].bitcast(I32))

        def deal(name, src, dtype, t0, t1, tag=None):
            dealt = sb(name, [P, (t1 - t0) * P], dtype, tag=tag)
            nc.vector.tensor_copy(
                dealt[:].rearrange("p (t a i) -> p a t i", t=t1 - t0, i=4),
                src.rearrange("p (a i t) -> p a t i", t=PACK, i=4)[:, :, t0:t1, :],
            )
            return [dealt[:, t * P : (t + 1) * P] for t in range(t1 - t0)]

        picked1 = sb("picked1", [P, H + S], U8, tag="picked")
        nc.vector.tensor_copy(picked1[:, H : H + S], x_sc[:].indirect(offs_t[:]))
        nc.vector.tensor_copy(picked1[:, 0:H], d_sc[:].indirect(k1_t[:]))
        place_rows(placed1, picked1, [nc.sync, nc.scalar])
        xq_w = sb("xq_w", [P, S], U32)
        nc.vector.tensor_copy(xq_w[:], x_w[:].indirect(offs_t[:]))
        w1_picked = sb("w1_picked", [P, H], U32)
        nc.vector.tensor_copy(w1_picked[:], d_w[:].indirect(k1_t[:]))
        w1_sc = deal("w1_sc_0", placed1[:, 0:H], U8, 0, 1)
        w1_w = deal("w1_w_0", w1_picked[:], U32, 0, 1)
        w1_sc = w1_sc + deal("w1_sc_rest", placed1[:, 0:H], U8, 1, PACK)
        w1_w = w1_w + deal("w1_w_rest", w1_picked[:], U32, 1, PACK)

        h_win = [sb(f"h_win{t}", [P, S], F32) for t in range(PACK)]
        plus_a = [sb(f"plus_a{t}", [P, HALF], F32) for t in range(PACK)]
        minus_a = sb("minus_a", [P, PACK, HALF], F32)
        plus_b = sb("plus_b", [P, PACK, HALF], F32)
        acc1 = [psum.tile([P, S], F32, name=f"acc1_{t}", tag=f"bank{t}") for t in range(PACK)]
        for t in range(PACK):
            nc.tensor.matmul_mx(
                acc1[t][:], lhsT=w1_w[t].bitcast(FP8X4), lhsT_scale=w1_sc[t],
                rhs=xq_w[:].bitcast(FP8X4), rhs_scale=placed1[:, H : H + S], start=True, stop=True,
            )
            nc.scalar.activation(h_win[t][:], acc1[t][:], ACT.Copy, scale=gain[:, t : t + 1])
            nc.scalar.copy(plus_a[t][:], acc1[t][:, 0:HALF])
            nc.scalar.activation(minus_a[:, t, :], acc1[t][:, 0:HALF], ACT.Copy, scale=-1.0)
        for t in range(PACK):
            nc.scalar.copy(plus_b[:, t, :], acc1[t][:, HALF:S])

        picked2 = sb("picked2", [P, H], U8)
        nc.vector.tensor_copy(picked2[:], d_sc[:].indirect(k2_t[:]))
        place_rows(placed2, picked2, [nc.sync])
        w2_picked = sb("w2_picked", [P, H], U32, tag="picked")
        nc.vector.tensor_copy(w2_picked[:], d_w[:].indirect(k2_t[:]))
        w2_w = deal("w2_w_0", w2_picked[:], U32, 0, 1)
        w2_sc = deal("w2_sc_0", placed2[:], U8, 0, 1)

        h2_win = [sb(f"h2_win{t}", [P, S], F32) for t in range(PACK)]
        z_bf = [sb(f"z_bf{n}", [P, P, PACK], BF16) for n in range(4)]
        z_w = sb("z_w", [P, S], U32)
        z_sc = sb("z_sc", [P, S], U8)
        per = HALF // 16

        def quantize_z(n):
            cols = slice(n * P, (n + 1) * P)
            nc.vector.quantize_mx(z_w[:, cols].bitcast(FP8X4), z_sc[:, cols], z_bf[n][:].rearrange("p c t -> p (c t)"))

        def second_product(t, at, width, bank):
            acc2 = psum.tile([P, width], F32, name=f"acc2_{t}_{at}", tag=f"bank{bank}")
            nc.tensor.matmul_mx(
                acc2[:], lhsT=w2_w[t].bitcast(FP8X4), lhsT_scale=w2_sc[t],
                rhs=z_w[:, at : at + width].bitcast(FP8X4), rhs_scale=z_sc[:, at : at + width], start=True, stop=True,
            )
            nc.scalar.activation(h2_win[t][:, at : at + width], acc2[:], ACT.Copy, scale=0.0625)

        first = sb("first", [P, PACK, HALF], F32)
        turned = [psum.tile([P, PACK, P], F32, name=f"turned{b}", tag=f"bank{PACK + b}") for b in range(2)]
        for t in range(PACK):
            nc.vector.tensor_copy(first[:, t, :], h_win[t][:].indirect(n1_t[:, per : 2 * per]))
            at_n2 = sb(f"at_n2_{t}", [P, HALF], F32)
            at_n1 = sb(f"at_n1_{t}", [P, HALF], F32)
            nc.vector.tensor_tensor(at_n2[:], h_win[t][:].indirect(n2_t[:, 0:per]), plus_a[t][:], ALU.mult)
            nc.vector.tensor_tensor(at_n1[:], h_win[t][:].indirect(n1_t[:, 0:per]), minus_a[:, t, :], ALU.mult)
            for b in range(2):
                cols = slice(b * P, (b + 1) * P)
                nc.tensor.matmul(turned[b][:, t, :], at_n2[:, cols], ident[:], start=True, stop=False, is_transpose=True)
                nc.tensor.matmul(turned[b][:, t, :], at_n1[:, cols], ident[:], start=False, stop=True, is_transpose=True)
        for b in range(2):
            pairs = sb(f"pairs{b}", [P, 2, P, 2], BF16)
            nc.scalar.copy(pairs[:], turned[b][:].rearrange("j (u e) p -> j u p e", e=2))
            words = pairs[:].rearrange("j u p e -> j (u p e)").bitcast(F32)
            back = psum.tile([P, 2, P], F32, name=f"back{b}", tag=f"bank{6 + b}")
            for u in range(2):
                nc.tensor.transpose(back[:, u, :], words[:, u * P : (u + 1) * P], ident[:])
            nc.scalar.copy(
                z_bf[b][:].rearrange("p c t -> p (c t)").bitcast(F32).rearrange("p (j u) -> p j u", u=2),
                back[:].rearrange("p u j -> p j u"),
            )
        diff = sb("diff", [P, PACK, HALF], F32, tag="minus_a")
        for t in range(PACK):
            nc.vector.tensor_tensor(diff[:, t, :], h_win[t][:].indirect(n2_t[:, per : 2 * per]), first[:, t, :], ALU.subtract)
        for b in range(2):
            cols = slice(b * P, (b + 1) * P)
            nc.vector.tensor_tensor(
                z_bf[2 + b][:].rearrange("p (a i) t -> p a t i", i=2),
                diff[:, :, cols].rearrange("p t (a i) -> p a t i", i=2),
                plus_b[:, :, cols].rearrange("p t (a i) -> p a t i", i=2),
                ALU.mult,
            )
        for n, bank in ((2, 0), (3, 1), (0, 4), (1, 5)):
            quantize_z(n)
            second_product(0, n * P, P, bank)
        w2_w = w2_w + deal("w2_w_rest", w2_picked[:], U32, 1, PACK, tag="z_bf1")
        w2_sc = w2_sc + deal("w2_sc_rest", placed2[:], U8, 1, PACK, tag="z_bf0")
        for t, bank in ((1, 2), (2, 3), (3, 6)):
            second_product(t, 0, S, bank)

        pa = [sb(f"pa{t}", [P, W], F32) for t in range(PACK)]
        gap = [sb(f"gap{t}", [P, W], F32) for t in range(PACK)]
        up = [sb(f"up{t}", [P, W], F32) for t in range(PACK)]
        neg = [sb(f"neg{t}", [P, W], F32) for t in range(PACK)]
        down = [sb(f"down{t}", [P, W], F32) for t in range(PACK)]
        y = [sb(f"y{t}", [P, S], F32) for t in range(PACK)]
        y_bf = sb("y_bf", [P, S, PACK], BF16)
        y_w = sb("y_w", [P, S], U32)
        y_sc = sb("y_sc", [P, S], U8)
        out_rows = out_0.rearrange("(p t) c -> p t c", t=PACK)

        def fetch_pair(t):
            halves = [(slice(c * P, (c + 1) * P), slice(c * P // 16, (c + 1) * P // 16)) for c in range(2)]
            for cols, entries in halves:
                nc.vector.tensor_copy(pa[t][:, cols], h2_win[t][:].indirect(n3_t[:, entries]))
            for cols, entries in halves:
                nc.vector.tensor_tensor(gap[t][:, cols], h2_win[t][:].indirect(n4_t[:, entries]), pa[t][:, cols], ALU.subtract)

        def rise(t):
            nc.scalar.activation(up[t][:], gap[t][:], ACT.Relu)

        def fall(t):
            nc.scalar.activation(neg[t][:], gap[t][:], ACT.Relu, scale=-1.0)
            nc.scalar.activation(down[t][:], neg[t][:], ACT.Copy, scale=-1.0)

        def put_larger(t):
            nc.vector.tensor_tensor(y[t][:].indirect(n3_t[:]), pa[t][:], up[t][:], ALU.add)

        def put_smaller(t):
            nc.vector.tensor_tensor(y[t][:].indirect(n4_t[:]), pa[t][:], down[t][:], ALU.add)
            nc.sync.dma_start(out_rows[:, t, :], y[t][:])

        for t in range(PACK):
            fetch_pair(t)
        rise(0)
        for t in range(1, PACK):
            rise(t)
            fall(t - 1)
        fall(PACK - 1)
        put_larger(0)
        put_larger(1)
        put_smaller(0)
        nc.scalar.copy(y_bf[:, :, 0], y[0][:])
        put_larger(2)
        put_smaller(1)
        nc.scalar.copy(y_bf[:, :, 1], y[1][:])
        put_larger(3)
        put_smaller(2)
        split = S - P
        for cols in (slice(0, HALF), slice(HALF, split)):
            width = cols.stop - cols.start
            nc.scalar.copy(y_bf[:, cols, 2:4], y[2][:, cols].unsqueeze(2).to_broadcast([P, width, 2]))
        nc.scalar.copy(y_bf[:, split:S, 2], y[2][:, split:S])
        put_smaller(3)
        words_out = out_1[0].rearrange("p c r -> p (c r)").bitcast(I32)
        for cols in (slice(0, HALF), slice(HALF, split)):
            nc.vector.tensor_copy(y_bf[:, cols, 3], y[3][:, cols])
        nc.scalar.copy(y_bf[:, split:S, 3], y[3][:, split:S])
        for c in range(2):
            cols = slice(c * HALF, (c + 1) * HALF)
            nc.vector.quantize_mx(y_w[:, cols].bitcast(FP8X4), y_sc[:, cols], y_bf[:, cols, :].rearrange("p c t -> p (c t)"))
            nc.sync.dma_start(words_out[:, cols], y_w[:, cols].bitcast(I32))
        scales_out = out_2[0].bitcast(I32)
        for q in range(4):
            queue = nc.scalar if q % 2 == 0 else nc.sync
            queue.dma_start(scales_out[4 * q : 4 * q + 4, :], y_sc[32 * q : 32 * q + 4, :].bitcast(I32))
